import numpy as np
import ml_dtypes


def mxq(x, axis, fmt="e4m3"):
    dtype, down = {"e4m3": (ml_dtypes.float8_e4m3fn, 7), "e5m2": (ml_dtypes.float8_e5m2, 14)}[fmt]
    v = np.moveaxis(np.asarray(x, np.float32).astype(ml_dtypes.bfloat16).astype(np.float64), axis, -1)
    blocks = v.reshape(v.shape[:-1] + (-1, 32))
    amax = np.abs(blocks).max(-1, keepdims=True)
    byte = np.maximum(np.where(amax > 0, np.frexp(amax)[1] - 1 + 127, 0) - down, 1)
    scale = np.exp2(byte - 127.0)
    codes = (blocks / scale).astype(np.float32).astype(dtype).astype(np.float64)
    return np.moveaxis((codes * scale).reshape(v.shape), -1, axis)


WIDE = False


def mx_kscale(k):
    if not WIDE:
        return np.ones(k)
    levels = np.array([10, -10, 5, -5, 0])
    if k % 512:
        return np.exp2(np.random.permutation(np.resize(levels, k // 32))).repeat(32)
    a = np.empty((k // 512, 16))
    for p in range(k // 512):
        a[p, :8] = np.random.permutation(np.resize(levels, 8))
        for g in range(8):
            far = levels[np.abs(levels - a[p, g]) >= 10]
            a[p, g + 8] = far[np.random.randint(len(far))]
    return np.exp2(a.ravel()).repeat(32)


def f64(x):
    return np.asarray(x).astype(np.float64)


def striped(idx):
    return np.tile(idx.reshape(-1, 16).T, (8, 1)).astype(np.uint16)


def unstriped(offs):
    return offs[:16].T.reshape(-1).astype(np.int64)


E2M1 = np.array([0.0, 0.5, 1.0, 1.5, 2.0, 3.0, 4.0, 6.0, -0.0, -0.5, -1.0, -1.5, -2.0, -3.0, -4.0, -6.0])


def pack_weight(w, fmt):
    k, n = w.shape
    w = f64(np.asarray(w, np.float32).astype(ml_dtypes.bfloat16)).reshape(k // 32, 32, n)
    amax = np.abs(w).max(1)
    if fmt == "e4m3":
        byte = np.frexp(amax)[1] - 1 + 127 - 7
    else:
        mant, ex = np.frexp(amax / 6.0)
        byte = np.where(mant > 0.5, ex, ex - 1) + 127
    byte = np.clip(np.where(amax > 0, byte, 1), 1, 254)
    scaled = (w * np.exp2(127.0 - byte)[:, None, :]).reshape(k, n).astype(np.float32)
    by_word = np.ascontiguousarray(scaled.reshape(k // 512, 128, 4, n).transpose(0, 1, 3, 2))
    if fmt == "e4m3":
        words = by_word.astype(ml_dtypes.float8_e4m3fn).view(np.uint8)
    else:
        c = by_word.astype(ml_dtypes.float4_e2m1fn).view(np.uint8) & 0xF
        words = (c[..., 0::2] | (c[..., 1::2] << 4)).reshape(k // 512, 128, 2 * n)
    return np.ascontiguousarray(words), np.ascontiguousarray(byte.astype(np.uint8).reshape(k // 512, 16, n))


def unpack_weight(words, scales, fmt):
    g, _, n = scales.shape
    words = np.ascontiguousarray(words).reshape(g, 128, n, -1)
    if fmt == "e4m3":
        vals = words.view(ml_dtypes.float8_e4m3fn).astype(np.float64)
    else:
        nib = np.empty((g, 128, n, 4), np.uint8)
        nib[..., 0::2] = words & 0xF
        nib[..., 1::2] = words >> 4
        vals = E2M1[nib]
    vals = vals * np.repeat(np.exp2(scales.astype(np.float64) - 127.0), 8, axis=1)[..., None]
    return vals.transpose(0, 1, 3, 2).reshape(g * 512, n)


def gelu(v):
    return 0.5 * v * (1.0 + np.tanh(np.sqrt(2.0 / np.pi) * (v + 0.044715 * v**3)))


def striped8(idx):
    return np.concatenate([v.reshape(-1, 16).T for v in idx]).astype(np.uint16)


def unstriped8(offs):
    return np.stack([offs[16 * g:16 * g + 16].T.reshape(-1) for g in range(8)]).astype(np.int64)


def runs(v, idx8):
    k = np.arange(v.shape[0])
    return v[k[:, None], idx8[k % 512 // 64]]


def bf(x):
    return np.asarray(x, np.float32).astype(ml_dtypes.bfloat16)


def planes(Y):
    n, m = Y.shape
    b = f64(bf(Y)).reshape(n // 32, 32, m)
    amax = np.abs(b).max(1)
    byte = np.clip(np.where(amax > 0, np.frexp(amax)[1] - 1 + 127 - 7, 1), 1, 254)
    codes = (b * np.exp2(127.0 - byte)[:, None, :]).reshape(n, m).astype(np.float32).astype(ml_dtypes.float8_e4m3fn).view(np.uint8)
    words = codes.reshape(n // 512, 128, 4, m).transpose(0, 1, 3, 2)
    return np.ascontiguousarray(words), np.ascontiguousarray(byte.astype(np.uint8).reshape(n // 512, 16, m))


T, S, P, K, H, N = 2048, 1024, 512, 1024, 512, 1024

def setup_inputs():
    n = np.random.standard_normal
    s = mx_kscale(K)[:, None]
    u = mx_kscale(H)[:, None]
    d = {}
    d["tab_words"], d["tab_scales"] = pack_weight(n((K, T)) * s, "e4m3")
    d["offs"] = striped8(np.stack([np.random.permutation(T)[:S] for _ in range(8)]))
    d["pos1"] = striped(np.random.permutation(S)[:P])
    d["pos2"] = striped(np.random.permutation(S)[:P])
    d["w1"] = (n((K, H)) / K**0.5 / s * u.T).astype(np.float32)
    d["w2"] = (n((K, H)) / K**0.5 / s * u.T).astype(np.float32)
    d["w3_words"], d["w3_scales"] = pack_weight(n((K, H)) / K**0.5 / s * u.T, "e2m1")
    d["w4_words"], d["w4_scales"] = pack_weight(n((H, N)) / H**0.5 / u, "e4m3")
    d["gain"] = np.exp(0.8 * n(N)).astype(np.float32)
    return d

def reference(tab_words, tab_scales, offs, pos1, pos2, w1, w2, w3_words, w3_scales, w4_words, w4_scales, gain):
    v = runs(unpack_weight(tab_words, tab_scales, "e4m3"), unstriped8(offs))
    pressing = mxq(f64(w1), 0, "e4m3").T @ v
    circling = mxq(f64(w2), 0, "e4m3").T @ v
    centre = unpack_weight(w3_words, w3_scales, "e2m1").T @ v
    h = np.maximum(pressing, circling) - centre
    x = np.abs(h[:, unstriped(pos1)] - h[:, unstriped(pos2)])
    y = unpack_weight(w4_words, w4_scales, "e4m3").T @ mxq(x, 0, "e4m3")
    y = f64(gain)[:, None] * y
    words, scales = planes(y)
    return y, words, scales

from contextlib import ExitStack

import concourse.mybir as mybir

T, S, PAIRS, K, H, N = 2048, 1024, 512, 1024, 512, 1024
FLOPS = 2 * (3 * K * H * S + H * N * PAIRS)

F32 = mybir.dt.float32
BF16 = mybir.dt.bfloat16
I32 = mybir.dt.int32
U32 = mybir.dt.uint32
U16 = mybir.dt.uint16
U8 = mybir.dt.uint8
FP8X4 = mybir.dt.float8_e4m3fn_x4
FP4X4 = mybir.dt.float4_e2m1fn_x4
ALU = mybir.AluOpType
ACT = mybir.ActivationFunctionType

P = 128
PACK = 4
K_PASS = P * PACK
PASSES = K // K_PASS
HALF = 512
HALVES = S // HALF
GROUPS = N // K_PASS
CHUNKS = [128,128,128,128]
GP_SUBS = 4
V_INT_FROM = 2


def tile_list_octagon_exchange_features_kernel(
    tc, tab_words, tab_scales, offs, pos1, pos2, w1, w2, w3_words, w3_scales, w4_words, w4_scales, gain,
    out_0, out_1, out_2,
):
    nc = tc.nc
    with ExitStack() as ctx:
        keep = ctx.enter_context(tc.tile_pool(name="keep", bufs=1))
        psum = ctx.enter_context(tc.psum_pool(name="psum", bufs=8))

        def tile(name, shape, dtype):
            return keep.tile(shape, dtype, name=name, align_bytes=64)

        offs_t = tile("offs_t", [P, S // 16], U16)
        pos1_t = tile("pos1_t", [P, PAIRS // 16], U16)
        pos2_t = tile("pos2_t", [P, PAIRS // 16], U16)
        def shared(tag, name, shape, dtype):
            return keep.tile(shape, dtype, name=name, tag=tag, align_bytes=64)

        tab_sc = shared("slot0", "tab_sc", [P, T], U8)
        v_sc = tile("v_sc", [P, PASSES * S], U8)
        w3s_raw = shared("slot4", "w3s_raw", [P, PASSES * H], U8)
        nc.gpsimd.memset(tab_sc[:].bitcast(I32), 0)
        nc.gpsimd.memset(w3s_raw[:].bitcast(I32), 0)

        gain_t = tile("gain_t", [P, GROUPS, PACK], F32)
        nc.sync.dma_start(offs_t[:], offs)
        nc.sync.dma_start(pos1_t[:], pos1)
        nc.sync.dma_start(pos2_t[:], pos2)
        w3_raw = tile("w3_raw", [P, PASSES * 2 * H], U8)
        nc.sync.dma_start(
            w3_raw[:].bitcast(I32).rearrange("p (a c) -> p a c", a=PASSES),
            w3_words.rearrange("a p c -> p a c").bitcast(I32),
        )
        nc.scalar.dma_start(tab_sc[0:P:4, :].bitcast(I32), tab_scales.rearrange("a q c -> q a c").bitcast(I32))

        tab_w = [shared("slot%d" % (2 + a), "tab_w%d" % a, [P, T], U32) for a in range(PASSES)]
        for a in range(PASSES):
            nc.sync.dma_start(tab_w[a][:].bitcast(I32), tab_words[a].rearrange("p t i -> p (t i)").bitcast(I32))
        for q in range(4):
            nc.gpsimd.dma_start(
                w3s_raw[32 * q : 32 * q + 4, :].bitcast(I32).rearrange("r (a c) -> r a c", a=PASSES),
                w3_scales[:, 4 * q : 4 * q + 4, :].rearrange("a r c -> r a c").bitcast(I32),
            )
        nc.gpsimd.memset(v_sc[:].bitcast(I32), 0)

        def rows(w, a):
            return w[a * K_PASS : (a + 1) * K_PASS, :].rearrange("(p j) c -> p j c", j=PACK)

        picked_sc = shared("slot1", "picked_sc", [P, S], U8)
        nc.vector.tensor_copy(picked_sc[:], tab_sc[:].indirect(offs_t[:]))
        for q in range(4):
            nc.sync.dma_start(
                v_sc[32 * q : 32 * q + 4, :].bitcast(I32), picked_sc[32 * q : 32 * q + 32 : 4, :].bitcast(I32)
            )
        w_raw = {}
        for a in range(PASSES):
            w_raw["w1", a] = [shared("slot%d" % a, "w1_raw%d" % a, [P, PACK, H], F32)]
            nc.sync.dma_start(w_raw["w1", a][0][:], rows(w1, a))

        v_w = {}
        w3_w = tile("w3_w", [P, PASSES * 2 * H], U8)
        w3_sc = tile("w3_sc", [P, PASSES * H], U8)
        nc.vector.tensor_copy(
            w3_w[:].bitcast(U16).rearrange("p (a t m) -> p a m t", a=PASSES, t=PACK),
            w3_raw[:].bitcast(U16).rearrange("p (a m t) -> p a m t", a=PASSES, t=PACK),
        )
        for hf in range(HALVES):
            for a in range(PASSES):
                v_w[a, hf] = tile("v_w%d_%d" % (a, hf), [P, HALF], U32)
                nc.vector.tensor_copy(v_w[a, hf][:], tab_w[a][:].indirect(offs_t[:, hf * 32 : (hf + 1) * 32]))
        nc.gpsimd.tensor_copy(
            w3_sc[:].rearrange("p (a t m) -> p a t m", a=PASSES, t=PACK),
            w3s_raw[:].rearrange("p (a m t) -> p a t m", a=PASSES, t=PACK),
        )
        w4s_raw = shared("slot4", "w4s_raw", [P, K_PASS], U8)
        nc.gpsimd.memset(w4s_raw[:].bitcast(I32), 0)
        for q in range(4):
            nc.gpsimd.dma_start(
                w4s_raw[32 * q : 32 * q + 8, :].bitcast(I32),
                w4_scales[0, 4 * q : 4 * q + 4, :].rearrange("r (g c) -> g r c", g=GROUPS).bitcast(I32),
            )
        nc.scalar.dma_start(gain_t[:], gain.rearrange("(g p t) -> p g t", g=GROUPS, t=PACK))

        w_raw["w2", 0] = [shared("slot2", "w2_raw0", [P, PACK, H], F32)]
        nc.sync.dma_start(w_raw["w2", 0][0][:], rows(w2, 0))
        w4_sc = tile("w4_sc", [P, K_PASS], U8)
        nc.gpsimd.tensor_copy(
            w4_sc[:].rearrange("p (t m) -> p t m", t=PACK), w4s_raw[:].rearrange("p (m t) -> p t m", t=PACK)
        )

        banks = [(t, hf) for t in range(PACK) for hf in range(HALVES)]

        def product(lhs, lhs_sc, t, hf):
            acc = psum.tile([P, HALF], F32, name="acc")
            for a in range(PASSES):
                nc.tensor.matmul_mx(
                    out=acc[:],
                    lhsT=lhs(a, t),
                    lhsT_scale=lhs_sc(a, t),
                    rhs=v_w[a, hf][:].bitcast(FP8X4),
                    rhs_scale=v_sc[:, a * S + hf * HALF : a * S + (hf + 1) * HALF],
                    start=(a == 0),
                    stop=(a == PASSES - 1),
                )
            return acc

        w_codes, w_sc, rounded = {}, {}, {}

        def cast(name, a, copy):
            rounded[name, a] = tile("%s_bf%d" % (name, a), [P, PACK * H], BF16)
            dst = rounded[name, a][:].rearrange("p (t m j) -> p m j t", t=PACK, j=PACK)
            parts = w_raw[name, a]
            width = P // len(parts)
            for i, part in enumerate(parts):
                copy(dst[:, i * width : (i + 1) * width], part[:].rearrange("p j (m t) -> p m j t", t=PACK))

        def quantise(name, a, parts=1):
            w_codes[name, a] = tile("%s_codes%d" % (name, a), [P, H], U32)
            w_sc[name, a] = tile("%s_sc%d" % (name, a), [P, H], U8)
            width = H // parts
            for i in range(parts):
                cols = slice(i * width, (i + 1) * width)
                nc.vector.quantize_mx(
                    out=w_codes[name, a][:, cols].bitcast(FP8X4),
                    scales=w_sc[name, a][:, cols],
                    in_=rounded[name, a][:, PACK * i * width : PACK * (i + 1) * width],
                )

        cast("w1", 0, nc.scalar.copy)
        centre = {}
        for hf in range(HALVES):
            for t in range(PACK):
                acc = product(
                    lambda a, t: w3_w[:, 2 * (a * H + P * t) : 2 * (a * H + P * (t + 1))].bitcast(FP4X4),
                    lambda a, t: w3_sc[:, a * H + P * t : a * H + P * (t + 1)],
                    t,
                    hf,
                )
                centre[t, hf] = tile("centre%d_%d" % (t, hf), [P, HALF], F32)
                nc.scalar.copy(centre[t, hf][:], acc[:])


        w_raw["w2", 1] = [
            shared("slot3", "w2_raw1a", [P, PACK, H // 2], F32),
            shared("slot0", "w2_raw1b", [P, PACK, H // 2], F32),
        ]
        for i in range(2):
            nc.sync.dma_start(w_raw["w2", 1][i][:], rows(w2, 1)[:, :, i * H // 2 : (i + 1) * H // 2])
        cast("w1", 1, nc.vector.tensor_copy)
        w4_raw = shared("slot1", "w4_raw", [P, N], I32)
        nc.sync.dma_start(w4_raw[:], w4_words[0].rearrange("p n i -> p (n i)").bitcast(I32))
        quantise("w1", 0)
        quantise("w1", 1)
        cast("w2", 0, nc.vector.tensor_copy)
        quantise("w2", 0)
        cast("w2", 1, nc.vector.tensor_copy)
        quantise("w2", 1, 2)

        def dense(name, t, hf):
            return product(
                lambda a, t: w_codes[name, a][:, P * t : P * (t + 1)].bitcast(FP8X4),
                lambda a, t: w_sc[name, a][:, P * t : P * (t + 1)],
                t,
                hf,
            )

        pressing = {}
        for t, hf in banks:
            acc = dense("w1", t, hf)
            pressing[t, hf] = tile("pressing%d_%d" % (t, hf), [P, HALF], F32)
            nc.scalar.copy(pressing[t, hf][:], acc[:])

        h = [tile("h%d" % t, [P, S], F32) for t in range(PACK)]
        larger = {}
        for i, (t, hf) in enumerate(banks):
            acc = dense("w2", t, hf)
            larger[t, hf] = tile("larger%d_%d" % (t, hf), [P, HALF], F32)
            nc.vector.tensor_tensor(larger[t, hf][:], acc[:], pressing[t, hf][:], ALU.max)
            if i < GP_SUBS:
                nc.gpsimd.tensor_tensor(
                    h[t][:, hf * HALF : (hf + 1) * HALF], larger[t, hf][:], centre[t, hf][:], ALU.subtract
                )
        for t, hf in banks[GP_SUBS:]:
            nc.vector.tensor_tensor(
                h[t][:, hf * HALF : (hf + 1) * HALF], larger[t, hf][:], centre[t, hf][:], ALU.subtract
            )

        w4_w = tile("w4_w", [P, N], I32)
        nc.vector.tensor_copy(
            w4_w[:].rearrange("p (g t m) -> p g m t", g=GROUPS, t=PACK),
            w4_raw[:].rearrange("p (g m t) -> p g m t", g=GROUPS, t=PACK),
        )

        y_codes = tile("y_codes", [P, GROUPS, PAIRS], U32)
        y_sc = tile("y_sc", [P, GROUPS, PAIRS], U8)
        out_rows = out_0.rearrange("(g p t) m -> g p t m", g=GROUPS, t=PACK)
        out_words = out_1.rearrange("g p m t -> p g (m t)").bitcast(I32)

        last = len(CHUNKS) - 1
        starts = [sum(CHUNKS[:i]) for i in range(len(CHUNKS))]
        closing, diff, x_bf, x_codes, x_sc, y = {}, {}, {}, {}, {}, {}

        def cols(ci):
            return slice(starts[ci] // 16, (starts[ci] + CHUNKS[ci]) // 16)

        def pick_closing(ci):
            closing[ci] = shared("closing", "closing%d" % ci, [P, PACK, CHUNKS[ci]], F32)
            for t in range(PACK):
                nc.vector.tensor_copy(closing[ci][:, t, :], h[t][:].indirect(pos2_t[:, cols(ci)]))

        def pick_opening(ci):
            diff[ci] = shared("pair%d" % ci, "diff%d" % ci, [P, PACK, CHUNKS[ci]], F32)
            for t in range(PACK):
                nc.vector.tensor_tensor(
                    diff[ci][:, t, :], h[t][:].indirect(pos1_t[:, cols(ci)]), closing[ci][:, t, :], ALU.subtract
                )

        def distance(ci):
            x_bf[ci] = shared("pair%d" % (ci + 1), "x_bf%d" % ci, [P, CHUNKS[ci] * PACK], BF16)
            nc.scalar.activation(
                x_bf[ci][:].rearrange("p (c i t) -> p c t i", i=4, t=PACK),
                diff[ci][:].rearrange("p t (c i) -> p c t i", i=4),
                ACT.Abs,
            )

        def second(ci):
            c0, width = starts[ci], CHUNKS[ci]
            x_codes = tile("x_codes%d" % ci, [P, width], U32)
            x_sc = tile("x_sc%d" % ci, [P, width], U8)
            nc.vector.quantize_mx(out=x_codes[:].bitcast(FP8X4), scales=x_sc[:], in_=x_bf[ci][:])
            per_bank = HALF // width
            for g in range(GROUPS):
                y[ci, g] = tile("y%d_%d" % (ci, g), [P, PACK, width], F32)
                for t0 in range(0, PACK, per_bank):
                    acc = psum.tile([P, HALF], F32, name="acc")
                    for t in range(t0, t0 + per_bank):
                        wc = slice(g * K_PASS + t * P, g * K_PASS + (t + 1) * P)
                        nc.tensor.matmul_mx(
                            out=acc[:, (t - t0) * width : (t - t0 + 1) * width],
                            lhsT=w4_w[:, wc].bitcast(FP8X4),
                            lhsT_scale=w4_sc[4 * g :, t * P : (t + 1) * P],
                            rhs=x_codes[:].bitcast(FP8X4),
                            rhs_scale=x_sc[:],
                            start=True,
                            stop=True,
                        )
                    if ci == last and g == 0:
                        nc.vector.tensor_tensor(
                            y[ci, g][:, t0 : t0 + per_bank, :],
                            acc[:].rearrange("p (t m) -> p t m", t=per_bank),
                            gain_t[:, g, t0 : t0 + per_bank].unsqueeze(2).to_broadcast([P, per_bank, width]),
                            ALU.mult,
                        )
                    else:
                        for t in range(t0, t0 + per_bank):
                            nc.scalar.activation(
                                y[ci, g][:, t, :], acc[:, (t - t0) * width : (t - t0 + 1) * width], ACT.Copy,
                                scale=gain_t[:, g, t : t + 1],
                            )
                nc.sync.dma_start(out_rows[g][:, :, c0 : c0 + width], y[ci, g][:])

        def planes(ci):
            c0, width = starts[ci], CHUNKS[ci]
            for g in range(GROUPS):
                y_bf = tile("y_bf%d_%d" % (ci, g), [P, width * PACK], BF16)
                dst = y_bf[:].rearrange("p (c i t) -> p c t i", i=4, t=PACK)
                src = y[ci, g][:].rearrange("p t (c i) -> p c t i", i=4)
                if ci >= V_INT_FROM:
                    nc.vector.tensor_copy(dst, src)
                else:
                    nc.scalar.copy(dst, src)
                nc.vector.quantize_mx(
                    out=y_codes[:, g, c0 : c0 + width].bitcast(FP8X4), scales=y_sc[:, g, c0 : c0 + width], in_=y_bf[:]
                )
            nc.sync.dma_start(out_words[:, :, c0 : c0 + width], y_codes[:, :, c0 : c0 + width].bitcast(I32))

        pick_closing(0)
        pick_opening(0)
        distance(0)
        for ci in range(last):
            pick_closing(ci + 1)
            second(ci)
            pick_opening(ci + 1)
            distance(ci + 1)
            planes(ci)
        second(last)
        planes(last)
        for q in range(4):
            (nc.sync, nc.scalar)[q % 2].dma_start(
                out_2[:, 4 * q : 4 * q + 4, :].rearrange("g r m -> r g m").bitcast(I32),
                y_sc[32 * q : 32 * q + 4, :, :].bitcast(I32),
            )
